import numpy as np
import ml_dtypes


def mxq(x, axis, fmt="e4m3"):
    dtype, down = {"e4m3": (ml_dtypes.float8_e4m3fn, 7), "e5m2": (ml_dtypes.float8_e5m2, 14)}[fmt]
    v = np.moveaxis(np.asarray(x, np.float32).astype(ml_dtypes.bfloat16).astype(np.float64), axis, -1)
    blocks = v.reshape(v.shape[:-1] + (-1, 32))
    amax = np.abs(blocks).max(-1, keepdims=True)
    byte = np.maximum(np.where(amax > 0, np.frexp(amax)[1] - 1 + 127, 0) - down, 1)
    scale = np.exp2(byte - 127.0)
    codes = (blocks / scale).astype(np.float32).astype(dtype).astype(np.float64)
    return np.moveaxis((codes * scale).reshape(v.shape), -1, axis)


WIDE = False


def mx_kscale(k):
    if not WIDE:
        return np.ones(k)
    levels = np.array([10, -10, 5, -5, 0])
    if k % 512:
        return np.exp2(np.random.permutation(np.resize(levels, k // 32))).repeat(32)
    a = np.empty((k // 512, 16))
    for p in range(k // 512):
        a[p, :8] = np.random.permutation(np.resize(levels, 8))
        for g in range(8):
            far = levels[np.abs(levels - a[p, g]) >= 10]
            a[p, g + 8] = far[np.random.randint(len(far))]
    return np.exp2(a.ravel()).repeat(32)


def f64(x):
    return np.asarray(x).astype(np.float64)


def striped8(idx):
    return np.asarray(idx).reshape(8, -1, 16).transpose(0, 2, 1).reshape(128, -1).astype(np.uint16)


def unstriped8(offs):
    return offs.reshape(8, 16, -1).transpose(0, 2, 1).reshape(8, -1).astype(np.int64)


def pick8(x, idx, run):
    r = np.arange(len(x))
    return x[r[:, None], idx[r % (8 * run) // run]]


E2M1 = np.array([0.0, 0.5, 1.0, 1.5, 2.0, 3.0, 4.0, 6.0, -0.0, -0.5, -1.0, -1.5, -2.0, -3.0, -4.0, -6.0])


def pack_weight(w, fmt):
    k, n = w.shape
    w = f64(np.asarray(w, np.float32).astype(ml_dtypes.bfloat16)).reshape(k // 32, 32, n)
    amax = np.abs(w).max(1)
    if fmt == "e4m3":
        byte = np.frexp(amax)[1] - 1 + 127 - 7
    else:
        mant, ex = np.frexp(amax / 6.0)
        byte = np.where(mant > 0.5, ex, ex - 1) + 127
    byte = np.clip(np.where(amax > 0, byte, 1), 1, 254)
    scaled = (w * np.exp2(127.0 - byte)[:, None, :]).reshape(k, n).astype(np.float32)
    by_word = np.ascontiguousarray(scaled.reshape(k // 512, 128, 4, n).transpose(0, 1, 3, 2))
    if fmt == "e4m3":
        words = by_word.astype(ml_dtypes.float8_e4m3fn).view(np.uint8)
    else:
        c = by_word.astype(ml_dtypes.float4_e2m1fn).view(np.uint8) & 0xF
        words = (c[..., 0::2] | (c[..., 1::2] << 4)).reshape(k // 512, 128, 2 * n)
    return np.ascontiguousarray(words), np.ascontiguousarray(byte.astype(np.uint8).reshape(k // 512, 16, n))


def unpack_weight(words, scales, fmt):
    g, _, n = scales.shape
    words = np.ascontiguousarray(words).reshape(g, 128, n, -1)
    if fmt == "e4m3":
        vals = words.view(ml_dtypes.float8_e4m3fn).astype(np.float64)
    else:
        nib = np.empty((g, 128, n, 4), np.uint8)
        nib[..., 0::2] = words & 0xF
        nib[..., 1::2] = words >> 4
        vals = E2M1[nib]
    vals = vals * np.repeat(np.exp2(scales.astype(np.float64) - 127.0), 8, axis=1)[..., None]
    return vals.transpose(0, 1, 3, 2).reshape(g * 512, n)


D, V, Q, I = 512, 2048, 128, 512


def setup_inputs():
    n = np.random.standard_normal
    idx = np.stack([np.random.permutation(V)[:I] for _ in range(8)])
    fd = mx_kscale(D)
    vocp = pack_weight(n((D, V)) / fd[:, None], "e4m3")
    return {
        "hid": (n((D, Q)) * 1.0 / np.sqrt(D) * fd[:, None]).astype(np.float32),
        "voc_words": vocp[0],
        "voc_scales": vocp[1],
        "sw": (np.random.uniform(0.5, 2.0, (1, I))).astype(np.float32),
        "dhid": (n((D, Q)) * 1.0 / np.sqrt(D) * fd[:, None]).astype(np.float32),
        "base": (0.5 * n((Q, V))).astype(np.float32),
        "offs": striped8(idx),
    }


def reference(hid, voc_words, voc_scales, sw, dhid, base, offs):
    idx = unstriped8(offs)
    vocu = unpack_weight(voc_words, voc_scales, "e4m3")
    hidq = mxq(f64(hid), 0, "e4m3")
    a = hidq.T @ vocu
    dhidq = mxq(f64(dhid), 0, "e4m3")
    ta = dhidq.T @ vocu
    m1 = np.max(a, axis=1, keepdims=True)
    px = np.exp(pick8(a, idx, 16) - m1)
    zl = np.sum(px, axis=1, keepdims=True)
    dzl = np.sum(f64(sw) / (px / zl + 0.001) * px / np.square(zl) * (-1.0), axis=1, keepdims=True)
    dpx = f64(sw) / (px / zl + 0.001) / zl + dzl
    xpx = pick8(ta, idx, 16) * px
    xzl = np.sum(xpx, axis=1, keepdims=True)
    xdzl = np.sum(((xpx - xzl * px / zl) / zl * f64(sw) / np.square(px / zl + 0.001) * (-1.0) * px + xpx * f64(sw) / (px / zl + 0.001) - xzl * zl * 2.0 * f64(sw) / (px / zl + 0.001) * px / np.square(zl)) / np.square(zl) * (-1.0), axis=1, keepdims=True)
    xdpx = ((xpx - xzl * px / zl) / zl * f64(sw) / np.square(px / zl + 0.001) * (-1.0) - xzl * f64(sw) / (px / zl + 0.001) / zl) / zl + xdzl
    xe1 = xdpx * px + xpx * dpx
    xs1 = np.zeros((Q, V))
    xs1[np.arange(Q)[:, None], idx[np.arange(Q) % 128 // 16]] = xe1
    y = xs1 + f64(base)
    return y

@@ -1,0 +1,205 @@
+import math
+from contextlib import ExitStack
+
+import concourse.mybir as mybir
+from concourse.masks import make_identity
+
+D, V, Q, I = 512, 2048, 128, 512
+FLOPS = 2 * 2 * D * V * Q
+
+F32 = mybir.dt.float32
+BF16 = mybir.dt.bfloat16
+I32 = mybir.dt.int32
+U32 = mybir.dt.uint32
+U16 = mybir.dt.uint16
+U8 = mybir.dt.uint8
+FP8X4 = mybir.dt.float8_e4m3fn_x4
+ALU = mybir.AluOpType
+ACT = mybir.ActivationFunctionType
+
+P = 128
+PACK = 4
+CHUNK = 512
+CHUNKS = V // CHUNK
+EPS = 0.001
+BITS_SLOPE = math.log(2.0) / 2.0**23
+OUT_CUTS = (0, 256, 768, 1280, 1792, 2048)
+
+
+def tile_attend_hvlistshare_heads_kernel(tc, hid, voc_words, voc_scales, sw, dhid, base, offs, out):
+    nc = tc.nc
+    with ExitStack() as ctx:
+        keep = ctx.enter_context(tc.tile_pool(name="keep", bufs=1))
+        psum = ctx.enter_context(tc.psum_pool(name="psum", bufs=1))
+
+        def column(name):
+            return keep.tile([P, 1], F32, name=name)
+
+        def slots(name):
+            return keep.tile([P, I], F32, name=name)
+
+        planes = keep.tile([P, CHUNK], U8, align_bytes=64)
+        nc.vector.memset(planes[:].bitcast(I32), 0)
+
+        hid_raw = keep.tile([P, PACK, Q], F32)
+        dhid_raw = keep.tile([P, PACK, Q], F32)
+        words = [keep.tile([P, CHUNK], U32, name="words%d" % c, align_bytes=64) for c in range(CHUNKS)]
+        words_hbm = voc_words.rearrange("z p n t -> p (z n t)").bitcast(I32)
+        scales_hbm = voc_scales.rearrange("z r n -> (z r) n").bitcast(I32)
+
+        def load_words(c):
+            nc.sync.dma_start(out=words[c][:].bitcast(I32), in_=words_hbm[:, c * CHUNK : (c + 1) * CHUNK])
+
+        nc.sync.dma_start(out=hid_raw[:], in_=hid.rearrange("(p j) q -> p j q", j=PACK))
+        for quad in range(4):
+            nc.scalar.dma_start(
+                out=planes[:].bitcast(I32)[32 * quad : 32 * quad + 16, :],
+                in_=scales_hbm[4 * quad : 4 * quad + 4, :].rearrange("r (c n) -> c r n", c=CHUNKS),
+            )
+        load_words(0)
+        nc.sync.dma_start(out=dhid_raw[:], in_=dhid.rearrange("(p j) q -> p j q", j=PACK))
+        for c in range(1, CHUNKS):
+            load_words(c)
+        offsets = keep.tile([P, I // 16], U16)
+        nc.sync.dma_start(offsets[:], offs)
+        sw_cols = keep.tile([P, PACK], F32)
+        nc.sync.dma_start(out=sw_cols[:], in_=sw.rearrange("o (p j) -> p (o j)", j=PACK))
+        base_sb = keep.tile([P, V], F32)
+        nc.sync.dma_start(out=base_sb[:], in_=base)
+
+        window = keep.tile([P, V], F32)
+        nc.vector.memset(window[:], 0.0)
+        identity = keep.tile([P, P], F32)
+        make_identity(nc, identity[:])
+
+        def quantize(raw, name):
+            grouped = keep.tile([P, Q, PACK], BF16, name=name + "_bf16", align_bytes=64)
+            nc.vector.tensor_copy(
+                out=grouped[:].rearrange("p (c i) j -> p c j i", i=4),
+                in_=raw[:].rearrange("p j (c i) -> p c j i", i=4),
+            )
+            codes = keep.tile([P, Q], U32, name=name + "_codes", align_bytes=64)
+            scales = keep.tile([P, Q], U8, name=name + "_scales", align_bytes=64)
+            nc.vector.quantize_mx(
+                out=codes[:].bitcast(FP8X4), scales=scales[:], in_=grouped[:].rearrange("p q j -> p (q j)")
+            )
+            return codes, scales
+
+        def scores(operand, c, name):
+            bank = psum.tile([P, CHUNK], F32, name=name)
+            nc.tensor.matmul_mx(
+                out=bank[:],
+                lhsT=operand[0][:].bitcast(FP8X4),
+                lhsT_scale=operand[1][:],
+                rhs=words[c][:].bitcast(FP8X4),
+                rhs_scale=planes[4 * c :, :],
+                start=True,
+                stop=True,
+            )
+            return bank
+
+        hid_q = quantize(hid_raw, "hid")
+        dhid_q = quantize(dhid_raw, "dhid")
+
+        a_sb = keep.tile([P, V], F32)
+        ta_sb = keep.tile([P, V], F32)
+        maxima = keep.tile([P, CHUNKS], F32)
+        for c in range(CHUNKS):
+            cols = slice(c * CHUNK, (c + 1) * CHUNK)
+            bank = scores(hid_q, c, "a%d" % c)
+            nc.vector.tensor_scalar(
+                out=a_sb[:, cols], in0=bank[:], scalar1=1.0, scalar2=None, op0=ALU.mult, op1=ALU.max,
+                accum_out=maxima[:, c : c + 1],
+            )
+            bank = scores(dhid_q, c, "ta%d" % (c % 3))
+            nc.scalar.activation(out=ta_sb[:, cols], in_=bank[:], func=ACT.Copy)
+
+        w_bank = psum.tile([P, PACK, P], F32)
+        for j in range(PACK):
+            nc.tensor.transpose(w_bank[:, j, :], sw_cols[:, j : j + 1].to_broadcast([P, P]), identity[:])
+        w_rows = w_bank[:].rearrange("q j k -> q k j")
+
+        def by4(t):
+            return t[:].rearrange("q (k j) -> q k j", j=PACK)
+
+        neg_m = column("neg_m")
+        nc.vector.tensor_reduce(out=neg_m[:], in_=maxima[:], axis=mybir.AxisListType.X, op=ALU.max, negate=True)
+        x = slots("x")
+        nc.vector.tensor_copy(out=x[:], in_=a_sb[:].indirect(offsets[:]))
+        t = slots("t")
+        nc.vector.tensor_copy(out=t[:], in_=ta_sb[:].indirect(offsets[:]))
+
+        half_m = column("half_m")
+        nc.scalar.activation(out=half_m[:], in_=neg_m[:], func=ACT.Copy, scale=-0.5, bias=0.5 * (math.log(EPS) + 0.5))
+        px = slots("px")
+        zl = column("zl")
+        nc.scalar.activation(out=px[:], in_=x[:], func=ACT.Exp, bias=neg_m[:], accum_out=zl[:])
+
+        bits = zl[:].bitcast(U32)
+        shift = column("shift")
+        nc.vector.memset(shift[:], 88.0)
+        minus2 = column("minus2")
+        nc.vector.memset(minus2[:], -2.0)
+        e0 = column("e0")
+        nc.scalar.activation(out=e0[:], in_=bits, func=ACT.Exp, scale=-BITS_SLOPE, bias=shift[:])
+        b0 = column("b0")
+        nc.scalar.activation(out=b0[:], in_=bits, func=ACT.Copy, scale=-BITS_SLOPE, bias=87.5)
+        sq0 = column("sq0")
+        nc.scalar.activation(out=sq0[:], in_=e0[:], func=ACT.Square, scale=zl[:], bias=minus2[:])
+        e1n = column("e1n")
+        nc.scalar.activation(out=e1n[:], in_=sq0[:], func=ACT.Exp, scale=0.5, bias=b0[:])
+        neg_y1 = column("neg_y1")
+        nc.scalar.activation(out=neg_y1[:], in_=sq0[:], func=ACT.Identity, scale=0.5, bias=b0[:])
+        sq = column("sq")
+        nc.scalar.activation(out=sq[:], in_=e1n[:], func=ACT.Square, scale=zl[:], bias=minus2[:])
+        c1 = column("c1")
+        nc.scalar.activation(out=c1[:], in_=neg_y1[:], func=ACT.Identity, scale=-0.5, bias=half_m[:])
+        beta = column("beta")
+        nc.scalar.activation(out=beta[:], in_=sq[:], func=ACT.Identity, scale=-0.25, bias=c1[:])
+        th = slots("th")
+        nc.scalar.activation(out=th[:], in_=x[:], func=ACT.Tanh, scale=-0.5, bias=beta[:])
+        one = column("one")
+        nc.vector.memset(one[:], 1.0)
+        sq2 = slots("sq2")
+        nc.scalar.activation(out=sq2[:], in_=th[:], func=ACT.Square, bias=one[:])
+
+        iz = column("iz")
+        nc.vector.reciprocal(out=iz[:], in_=zl[:])
+        ts = slots("ts")
+        tb = column("tb")
+        nc.vector.scalar_tensor_tensor(
+            out=ts[:], in0=t[:], scalar=iz[:], in1=px[:], op0=ALU.mult, op1=ALU.mult, accum_out=tb[:]
+        )
+        pu = slots("pu")
+        nc.vector.scalar_tensor_tensor(out=pu[:], in0=t[:], scalar=tb[:], in1=px[:], op0=ALU.subtract, op1=ALU.mult)
+        g2 = slots("g2")
+        an2 = column("an2")
+        nc.vector.scalar_tensor_tensor(
+            out=by4(g2), in0=by4(th), scalar=1.0, in1=w_rows, op0=ALU.subtract, op1=ALU.mult, accum_out=an2[:]
+        )
+        izh = column("izh")
+        nc.scalar.activation(out=izh[:], in_=iz[:], func=ACT.Copy, scale=0.5)
+        izm = column("izm")
+        nc.scalar.activation(out=izm[:], in_=iz[:], func=ACT.Copy, scale=0.25 / EPS)
+        niz = column("niz")
+        nc.scalar.activation(out=niz[:], in_=iz[:], func=ACT.Copy, scale=-1.0)
+        an = column("an")
+        nc.scalar.activation(out=an[:], in_=an2[:], func=ACT.Copy, scale=izh[:])
+        mz = slots("mz")
+        nc.vector.scalar_tensor_tensor(
+            out=by4(mz), in0=by4(sq2), scalar=izm[:], in1=w_rows, op0=ALU.mult, op1=ALU.mult
+        )
+        e1 = slots("e1")
+        hsum = column("hsum")
+        nc.vector.scalar_tensor_tensor(
+            out=e1[:], in0=mz[:], scalar=an[:], in1=pu[:], op0=ALU.add, op1=ALU.mult, accum_out=hsum[:]
+        )
+        n = slots("n")
+        nc.vector.tensor_scalar(out=n[:], in0=px[:], scalar1=hsum[:], scalar2=niz[:], op0=ALU.mult, op1=ALU.mult)
+        nc.vector.tensor_tensor(out=window[:].indirect(offsets[:]), in0=e1[:], in1=n[:], op=ALU.add)
+
+        for k in range(len(OUT_CUTS) - 1):
+            cols = slice(OUT_CUTS[k], OUT_CUTS[k + 1])
+            res = keep.tile([P, OUT_CUTS[k + 1] - OUT_CUTS[k]], F32, name="res%d" % k)
+            nc.vector.tensor_tensor(out=res[:], in0=window[:, cols], in1=base_sb[:, cols], op=ALU.add)
+            nc.sync.dma_start(out=out[:, cols], in_=res[:])

@@ -39,7 +39,7 @@ def tile_attend_hvlistshare_heads_kernel(tc, hid, voc_words, voc_scales, sw, dhi
             return keep.tile([P, I], F32, name=name)
 
         planes = keep.tile([P, CHUNK], U8, align_bytes=64)
-        nc.vector.memset(planes[:].bitcast(I32), 0)
+        nc.gpsimd.memset(planes[:].bitcast(I32), 0)
 
         hid_raw = keep.tile([P, PACK, Q], F32)
         dhid_raw = keep.tile([P, PACK, Q], F32)
@@ -56,9 +56,8 @@ def tile_attend_hvlistshare_heads_kernel(tc, hid, voc_words, voc_scales, sw, dhi
                 out=planes[:].bitcast(I32)[32 * quad : 32 * quad + 16, :],
                 in_=scales_hbm[4 * quad : 4 * quad + 4, :].rearrange("r (c n) -> c r n", c=CHUNKS),
             )
-        load_words(0)
         nc.sync.dma_start(out=dhid_raw[:], in_=dhid.rearrange("(p j) q -> p j q", j=PACK))
-        for c in range(1, CHUNKS):
+        for c in range(CHUNKS):
             load_words(c)
         offsets = keep.tile([P, I // 16], U16)
         nc.sync.dma_start(offsets[:], offs)
@@ -104,30 +103,37 @@ def tile_attend_hvlistshare_heads_kernel(tc, hid, voc_words, voc_scales, sw, dhi
         a_sb = keep.tile([P, V], F32)
         ta_sb = keep.tile([P, V], F32)
         maxima = keep.tile([P, CHUNKS], F32)
-        for c in range(CHUNKS):
-            cols = slice(c * CHUNK, (c + 1) * CHUNK)
+
+        def a_chunk(c):
             bank = scores(hid_q, c, "a%d" % c)
             nc.vector.tensor_scalar(
-                out=a_sb[:, cols], in0=bank[:], scalar1=1.0, scalar2=None, op0=ALU.mult, op1=ALU.max,
-                accum_out=maxima[:, c : c + 1],
+                out=a_sb[:, c * CHUNK : (c + 1) * CHUNK], in0=bank[:], scalar1=1.0, scalar2=None,
+                op0=ALU.mult, op1=ALU.max, accum_out=maxima[:, c : c + 1],
             )
-            bank = scores(dhid_q, c, "ta%d" % (c % 3))
-            nc.scalar.activation(out=ta_sb[:, cols], in_=bank[:], func=ACT.Copy)
 
-        w_bank = psum.tile([P, PACK, P], F32)
+        def ta_chunk(c):
+            bank = scores(dhid_q, c, "a0" if c == CHUNKS - 1 else "ta%d" % c)
+            nc.scalar.activation(out=ta_sb[:, c * CHUNK : (c + 1) * CHUNK], in_=bank[:], func=ACT.Copy)
+
+        for c in range(CHUNKS):
+            if c >= 2:
+                ta_chunk(c - 2)
+            a_chunk(c)
+
+        neg_m = column("neg_m")
+        nc.vector.tensor_reduce(out=neg_m[:], in_=maxima[:], axis=mybir.AxisListType.X, op=ALU.max, negate=True)
+        x = slots("x")
+        nc.vector.tensor_copy(out=x[:], in_=a_sb[:].indirect(offsets[:]))
+        ta_chunk(CHUNKS - 2)
+        ta_chunk(CHUNKS - 1)
+
+        w_bank = psum.tile([P, PACK, P], F32, name="a3")
         for j in range(PACK):
             nc.tensor.transpose(w_bank[:, j, :], sw_cols[:, j : j + 1].to_broadcast([P, P]), identity[:])
         w_rows = w_bank[:].rearrange("q j k -> q k j")
 
         def by4(t):
             return t[:].rearrange("q (k j) -> q k j", j=PACK)
-
-        neg_m = column("neg_m")
-        nc.vector.tensor_reduce(out=neg_m[:], in_=maxima[:], axis=mybir.AxisListType.X, op=ALU.max, negate=True)
-        x = slots("x")
-        nc.vector.tensor_copy(out=x[:], in_=a_sb[:].indirect(offsets[:]))
-        t = slots("t")
-        nc.vector.tensor_copy(out=t[:], in_=ta_sb[:].indirect(offsets[:]))
 
         half_m = column("half_m")
         nc.scalar.activation(out=half_m[:], in_=neg_m[:], func=ACT.Copy, scale=-0.5, bias=0.5 * (math.log(EPS) + 0.5))
@@ -158,44 +164,47 @@ def tile_attend_hvlistshare_heads_kernel(tc, hid, voc_words, voc_scales, sw, dhi
         nc.scalar.activation(out=beta[:], in_=sq[:], func=ACT.Identity, scale=-0.25, bias=c1[:])
         th = slots("th")
         nc.scalar.activation(out=th[:], in_=x[:], func=ACT.Tanh, scale=-0.5, bias=beta[:])
-        one = column("one")
-        nc.vector.memset(one[:], 1.0)
+        root = column("root")
+        nc.scalar.activation(out=root[:], in_=minus2[:], func=ACT.Copy, scale=-0.25 / math.sqrt(EPS))
         sq2 = slots("sq2")
-        nc.scalar.activation(out=sq2[:], in_=th[:], func=ACT.Square, bias=one[:])
+        nc.scalar.activation(out=sq2[:], in_=th[:], func=ACT.Square, scale=root[:], bias=root[:])
 
         iz = column("iz")
         nc.vector.reciprocal(out=iz[:], in_=zl[:])
+        t = slots("t")
+        nc.vector.tensor_copy(out=t[:], in_=ta_sb[:].indirect(offsets[:]))
         ts = slots("ts")
         tb = column("tb")
         nc.vector.scalar_tensor_tensor(
             out=ts[:], in0=t[:], scalar=iz[:], in1=px[:], op0=ALU.mult, op1=ALU.mult, accum_out=tb[:]
         )
+        factors = keep.tile([P, 2], F32)
+        nc.vector.memset(factors[:, 0:1], 0.5)
+        nc.vector.memset(factors[:, 1:2], -1.0)
+        iz2 = keep.tile([P, 2], F32)
+        nc.vector.tensor_scalar(out=iz2[:], in0=factors[:], scalar1=iz[:], scalar2=None, op0=ALU.mult)
         pu = slots("pu")
         nc.vector.scalar_tensor_tensor(out=pu[:], in0=t[:], scalar=tb[:], in1=px[:], op0=ALU.subtract, op1=ALU.mult)
+        wpu = slots("wpu")
+        nc.vector.tensor_tensor(out=by4(wpu), in0=by4(pu), in1=w_rows, op=ALU.mult)
         g2 = slots("g2")
         an2 = column("an2")
         nc.vector.scalar_tensor_tensor(
             out=by4(g2), in0=by4(th), scalar=1.0, in1=w_rows, op0=ALU.subtract, op1=ALU.mult, accum_out=an2[:]
         )
-        izh = column("izh")
-        nc.scalar.activation(out=izh[:], in_=iz[:], func=ACT.Copy, scale=0.5)
-        izm = column("izm")
-        nc.scalar.activation(out=izm[:], in_=iz[:], func=ACT.Copy, scale=0.25 / EPS)
-        niz = column("niz")
-        nc.scalar.activation(out=niz[:], in_=iz[:], func=ACT.Copy, scale=-1.0)
+        sneg = slots("x")
+        nc.scalar.activation(out=sneg[:], in_=px[:], func=ACT.Copy, scale=iz2[:, 1:2])
         an = column("an")
-        nc.scalar.activation(out=an[:], in_=an2[:], func=ACT.Copy, scale=izh[:])
-        mz = slots("mz")
-        nc.vector.scalar_tensor_tensor(
-            out=by4(mz), in0=by4(sq2), scalar=izm[:], in1=w_rows, op0=ALU.mult, op1=ALU.mult
-        )
-        e1 = slots("e1")
+        nc.scalar.activation(out=an[:], in_=an2[:], func=ACT.Copy, scale=iz2[:, 0:1])
+        h = slots("h")
         hsum = column("hsum")
         nc.vector.scalar_tensor_tensor(
-            out=e1[:], in0=mz[:], scalar=an[:], in1=pu[:], op0=ALU.add, op1=ALU.mult, accum_out=hsum[:]
+            out=h[:], in0=sq2[:], scalar=iz[:], in1=wpu[:], op0=ALU.mult, op1=ALU.mult, accum_out=hsum[:]
         )
+        e1 = slots("e1")
+        nc.vector.scalar_tensor_tensor(out=e1[:], in0=pu[:], scalar=an[:], in1=h[:], op0=ALU.mult, op1=ALU.add)
         n = slots("n")
-        nc.vector.tensor_scalar(out=n[:], in0=px[:], scalar1=hsum[:], scalar2=niz[:], op0=ALU.mult, op1=ALU.mult)
+        nc.scalar.activation(out=n[:], in_=sneg[:], func=ACT.Copy, scale=hsum[:])
         nc.vector.tensor_tensor(out=window[:].indirect(offsets[:]), in0=e1[:], in1=n[:], op=ALU.add)
 
         for k in range(len(OUT_CUTS) - 1):

@@ -52,7 +52,7 @@ def tile_attend_hvlistshare_heads_kernel(tc, hid, voc_words, voc_scales, sw, dhi
 
         nc.sync.dma_start(out=hid_raw[:], in_=hid.rearrange("(p j) q -> p j q", j=PACK))
         for quad in range(4):
-            nc.scalar.dma_start(
+            nc.sync.dma_start(
                 out=planes[:].bitcast(I32)[32 * quad : 32 * quad + 16, :],
                 in_=scales_hbm[4 * quad : 4 * quad + 4, :].rearrange("r (c n) -> c r n", c=CHUNKS),
             )
@@ -136,7 +136,7 @@ def tile_attend_hvlistshare_heads_kernel(tc, hid, voc_words, voc_scales, sw, dhi
             return t[:].rearrange("q (k j) -> q k j", j=PACK)
 
         half_m = column("half_m")
-        nc.scalar.activation(out=half_m[:], in_=neg_m[:], func=ACT.Copy, scale=-0.5, bias=0.5 * (math.log(EPS) + 0.5))
+        nc.scalar.activation(out=half_m[:], in_=neg_m[:], func=ACT.Copy, scale=-0.25, bias=0.25 * (math.log(EPS) - 1.0))
         px = slots("px")
         zl = column("zl")
         nc.scalar.activation(out=px[:], in_=x[:], func=ACT.Exp, bias=neg_m[:], accum_out=zl[:])
@@ -144,28 +144,32 @@ def tile_attend_hvlistshare_heads_kernel(tc, hid, voc_words, voc_scales, sw, dhi
         bits = zl[:].bitcast(U32)
         shift = column("shift")
         nc.vector.memset(shift[:], 88.0)
-        minus2 = column("minus2")
-        nc.vector.memset(minus2[:], -2.0)
         e0 = column("e0")
         nc.scalar.activation(out=e0[:], in_=bits, func=ACT.Exp, scale=-BITS_SLOPE, bias=shift[:])
-        b0 = column("b0")
-        nc.scalar.activation(out=b0[:], in_=bits, func=ACT.Copy, scale=-BITS_SLOPE, bias=87.5)
-        sq0 = column("sq0")
-        nc.scalar.activation(out=sq0[:], in_=e0[:], func=ACT.Square, scale=zl[:], bias=minus2[:])
-        e1n = column("e1n")
-        nc.scalar.activation(out=e1n[:], in_=sq0[:], func=ACT.Exp, scale=0.5, bias=b0[:])
-        neg_y1 = column("neg_y1")
-        nc.scalar.activation(out=neg_y1[:], in_=sq0[:], func=ACT.Identity, scale=0.5, bias=b0[:])
-        sq = column("sq")
-        nc.scalar.activation(out=sq[:], in_=e1n[:], func=ACT.Square, scale=zl[:], bias=minus2[:])
+        neg_z = column("neg_z")
+        nc.scalar.activation(out=neg_z[:], in_=zl[:], func=ACT.Copy, scale=-1.0)
+        b01 = column("b01")
+        nc.scalar.activation(out=b01[:], in_=bits, func=ACT.Copy, scale=-BITS_SLOPE, bias=89.0)
+        b02 = column("b02")
+        nc.scalar.activation(out=b02[:], in_=bits, func=ACT.Copy, scale=-BITS_SLOPE, bias=90.0)
+        e12 = keep.tile([P, 2], F32)
+        nc.scalar.activation(out=e12[:, 0:1], in_=e0[:], func=ACT.Exp, scale=neg_z[:], bias=b01[:])
+        b11 = column("b11")
+        nc.scalar.activation(out=b11[:], in_=e0[:], func=ACT.Identity, scale=neg_z[:], bias=b02[:])
+        half_z = column("half_z")
+        nc.scalar.activation(out=half_z[:], in_=zl[:], func=ACT.Copy, scale=0.5)
+        nc.scalar.activation(out=e12[:, 1:2], in_=e12[:, 0:1], func=ACT.Exp, scale=neg_z[:], bias=b11[:])
         c1 = column("c1")
-        nc.scalar.activation(out=c1[:], in_=neg_y1[:], func=ACT.Identity, scale=-0.5, bias=half_m[:])
+        nc.scalar.activation(out=c1[:], in_=b11[:], func=ACT.Identity, scale=-0.25, bias=half_m[:])
+        terms = keep.tile([P, 2], F32)
         beta = column("beta")
-        nc.scalar.activation(out=beta[:], in_=sq[:], func=ACT.Identity, scale=-0.25, bias=c1[:])
+        nc.scalar.activation(
+            out=terms[:], in_=e12[:], func=ACT.Identity, scale=half_z[:], bias=c1[:], accum_out=beta[:]
+        )
         th = slots("th")
         nc.scalar.activation(out=th[:], in_=x[:], func=ACT.Tanh, scale=-0.5, bias=beta[:])
         root = column("root")
-        nc.scalar.activation(out=root[:], in_=minus2[:], func=ACT.Copy, scale=-0.25 / math.sqrt(EPS))
+        nc.scalar.activation(out=root[:], in_=shift[:], func=ACT.Copy, scale=0.5 / math.sqrt(EPS) / 88.0)
         sq2 = slots("sq2")
         nc.scalar.activation(out=sq2[:], in_=th[:], func=ACT.Square, scale=root[:], bias=root[:])
 

import math
from contextlib import ExitStack

import concourse.mybir as mybir
from concourse.masks import make_identity

D, V, Q, I = 512, 2048, 128, 512
FLOPS = 2 * 2 * D * V * Q

F32 = mybir.dt.float32
BF16 = mybir.dt.bfloat16
I32 = mybir.dt.int32
U32 = mybir.dt.uint32
U16 = mybir.dt.uint16
U8 = mybir.dt.uint8
FP8X4 = mybir.dt.float8_e4m3fn_x4
ALU = mybir.AluOpType
ACT = mybir.ActivationFunctionType

P = 128
PACK = 4
CHUNK = 512
CHUNKS = V // CHUNK
EPS = 0.001
BITS_SLOPE = math.log(2.0) / 2.0**23
OUT_CUTS = (0, 256, 768, 1280, 1792, 2048)


def tile_attend_hvlistshare_heads_kernel(tc, hid, voc_words, voc_scales, sw, dhid, base, offs, out):
    nc = tc.nc
    with ExitStack() as ctx:
        keep = ctx.enter_context(tc.tile_pool(name="keep", bufs=1))
        psum = ctx.enter_context(tc.psum_pool(name="psum", bufs=1))

        def column(name):
            return keep.tile([P, 1], F32, name=name)

        def slots(name):
            return keep.tile([P, I], F32, name=name)

        planes = keep.tile([P, CHUNK], U8, align_bytes=64)
        nc.gpsimd.memset(planes[:].bitcast(I32), 0)

        hid_raw = keep.tile([P, PACK, Q], F32)
        dhid_raw = keep.tile([P, PACK, Q], F32)
        words = [keep.tile([P, CHUNK], U32, name="words%d" % c, align_bytes=64) for c in range(CHUNKS)]
        words_hbm = voc_words.rearrange("z p n t -> p (z n t)").bitcast(I32)
        scales_hbm = voc_scales.rearrange("z r n -> (z r) n").bitcast(I32)

        def load_words(c):
            nc.sync.dma_start(out=words[c][:].bitcast(I32), in_=words_hbm[:, c * CHUNK : (c + 1) * CHUNK])

        nc.sync.dma_start(out=hid_raw[:], in_=hid.rearrange("(p j) q -> p j q", j=PACK))
        for quad in range(4):
            nc.sync.dma_start(
                out=planes[:].bitcast(I32)[32 * quad : 32 * quad + 16, :],
                in_=scales_hbm[4 * quad : 4 * quad + 4, :].rearrange("r (c n) -> c r n", c=CHUNKS),
            )
        nc.sync.dma_start(out=dhid_raw[:], in_=dhid.rearrange("(p j) q -> p j q", j=PACK))
        for c in range(CHUNKS):
            load_words(c)
        offsets = keep.tile([P, I // 16], U16)
        nc.sync.dma_start(offsets[:], offs)
        sw_cols = keep.tile([P, PACK], F32)
        nc.sync.dma_start(out=sw_cols[:], in_=sw.rearrange("o (p j) -> p (o j)", j=PACK))
        base_sb = keep.tile([P, V], F32)
        nc.sync.dma_start(out=base_sb[:], in_=base)

        window = keep.tile([P, V], F32)
        nc.vector.memset(window[:], 0.0)
        identity = keep.tile([P, P], F32)
        make_identity(nc, identity[:])

        def quantize(raw, name):
            grouped = keep.tile([P, Q, PACK], BF16, name=name + "_bf16", align_bytes=64)
            nc.vector.tensor_copy(
                out=grouped[:].rearrange("p (c i) j -> p c j i", i=4),
                in_=raw[:].rearrange("p j (c i) -> p c j i", i=4),
            )
            codes = keep.tile([P, Q], U32, name=name + "_codes", align_bytes=64)
            scales = keep.tile([P, Q], U8, name=name + "_scales", align_bytes=64)
            nc.vector.quantize_mx(
                out=codes[:].bitcast(FP8X4), scales=scales[:], in_=grouped[:].rearrange("p q j -> p (q j)")
            )
            return codes, scales

        def scores(operand, c, name):
            bank = psum.tile([P, CHUNK], F32, name=name)
            nc.tensor.matmul_mx(
                out=bank[:],
                lhsT=operand[0][:].bitcast(FP8X4),
                lhsT_scale=operand[1][:],
                rhs=words[c][:].bitcast(FP8X4),
                rhs_scale=planes[4 * c :, :],
                start=True,
                stop=True,
            )
            return bank

        hid_q = quantize(hid_raw, "hid")
        dhid_q = quantize(dhid_raw, "dhid")

        a_sb = keep.tile([P, V], F32)
        ta_sb = keep.tile([P, V], F32)
        maxima = keep.tile([P, CHUNKS], F32)

        def a_chunk(c):
            bank = scores(hid_q, c, "a%d" % c)
            nc.vector.tensor_scalar(
                out=a_sb[:, c * CHUNK : (c + 1) * CHUNK], in0=bank[:], scalar1=1.0, scalar2=None,
                op0=ALU.mult, op1=ALU.max, accum_out=maxima[:, c : c + 1],
            )

        def ta_chunk(c):
            bank = scores(dhid_q, c, "a0" if c == CHUNKS - 1 else "ta%d" % c)
            nc.scalar.activation(out=ta_sb[:, c * CHUNK : (c + 1) * CHUNK], in_=bank[:], func=ACT.Copy)

        for c in range(CHUNKS):
            if c >= 2:
                ta_chunk(c - 2)
            a_chunk(c)

        neg_m = column("neg_m")
        nc.vector.tensor_reduce(out=neg_m[:], in_=maxima[:], axis=mybir.AxisListType.X, op=ALU.max, negate=True)
        x = slots("x")
        nc.vector.tensor_copy(out=x[:], in_=a_sb[:].indirect(offsets[:]))
        ta_chunk(CHUNKS - 2)
        ta_chunk(CHUNKS - 1)

        w_bank = psum.tile([P, PACK, P], F32, name="a3")
        for j in range(PACK):
            nc.tensor.transpose(w_bank[:, j, :], sw_cols[:, j : j + 1].to_broadcast([P, P]), identity[:])
        w_rows = w_bank[:].rearrange("q j k -> q k j")

        def by4(t):
            return t[:].rearrange("q (k j) -> q k j", j=PACK)

        half_m = column("half_m")
        nc.scalar.activation(out=half_m[:], in_=neg_m[:], func=ACT.Copy, scale=-0.25, bias=0.25 * (math.log(EPS) - 1.0))
        px = slots("px")
        zl = column("zl")
        nc.scalar.activation(out=px[:], in_=x[:], func=ACT.Exp, bias=neg_m[:], accum_out=zl[:])

        bits = zl[:].bitcast(U32)
        shift = column("shift")
        nc.vector.memset(shift[:], 88.0)
        e0 = column("e0")
        nc.scalar.activation(out=e0[:], in_=bits, func=ACT.Exp, scale=-BITS_SLOPE, bias=shift[:])
        neg_z = column("neg_z")
        nc.scalar.activation(out=neg_z[:], in_=zl[:], func=ACT.Copy, scale=-1.0)
        b01 = column("b01")
        nc.scalar.activation(out=b01[:], in_=bits, func=ACT.Copy, scale=-BITS_SLOPE, bias=89.0)
        b02 = column("b02")
        nc.scalar.activation(out=b02[:], in_=bits, func=ACT.Copy, scale=-BITS_SLOPE, bias=90.0)
        e12 = keep.tile([P, 2], F32)
        nc.scalar.activation(out=e12[:, 0:1], in_=e0[:], func=ACT.Exp, scale=neg_z[:], bias=b01[:])
        b11 = column("b11")
        nc.scalar.activation(out=b11[:], in_=e0[:], func=ACT.Identity, scale=neg_z[:], bias=b02[:])
        half_z = column("half_z")
        nc.scalar.activation(out=half_z[:], in_=zl[:], func=ACT.Copy, scale=0.5)
        nc.scalar.activation(out=e12[:, 1:2], in_=e12[:, 0:1], func=ACT.Exp, scale=neg_z[:], bias=b11[:])
        c1 = column("c1")
        nc.scalar.activation(out=c1[:], in_=b11[:], func=ACT.Identity, scale=-0.25, bias=half_m[:])
        terms = keep.tile([P, 2], F32)
        beta = column("beta")
        nc.scalar.activation(
            out=terms[:], in_=e12[:], func=ACT.Identity, scale=half_z[:], bias=c1[:], accum_out=beta[:]
        )
        th = slots("th")
        nc.scalar.activation(out=th[:], in_=x[:], func=ACT.Tanh, scale=-0.5, bias=beta[:])
        root = column("root")
        nc.scalar.activation(out=root[:], in_=shift[:], func=ACT.Copy, scale=0.5 / math.sqrt(EPS) / 88.0)
        sq2 = slots("sq2")
        nc.scalar.activation(out=sq2[:], in_=th[:], func=ACT.Square, scale=root[:], bias=root[:])

        iz = column("iz")
        nc.vector.reciprocal(out=iz[:], in_=zl[:])
        t = slots("t")
        nc.vector.tensor_copy(out=t[:], in_=ta_sb[:].indirect(offsets[:]))
        ts = slots("ts")
        tb = column("tb")
        nc.vector.scalar_tensor_tensor(
            out=ts[:], in0=t[:], scalar=iz[:], in1=px[:], op0=ALU.mult, op1=ALU.mult, accum_out=tb[:]
        )
        factors = keep.tile([P, 2], F32)
        nc.vector.memset(factors[:, 0:1], 0.5)
        nc.vector.memset(factors[:, 1:2], -1.0)
        iz2 = keep.tile([P, 2], F32)
        nc.vector.tensor_scalar(out=iz2[:], in0=factors[:], scalar1=iz[:], scalar2=None, op0=ALU.mult)
        pu = slots("pu")
        nc.vector.scalar_tensor_tensor(out=pu[:], in0=t[:], scalar=tb[:], in1=px[:], op0=ALU.subtract, op1=ALU.mult)
        wpu = slots("wpu")
        nc.vector.tensor_tensor(out=by4(wpu), in0=by4(pu), in1=w_rows, op=ALU.mult)
        g2 = slots("g2")
        an2 = column("an2")
        nc.vector.scalar_tensor_tensor(
            out=by4(g2), in0=by4(th), scalar=1.0, in1=w_rows, op0=ALU.subtract, op1=ALU.mult, accum_out=an2[:]
        )
        sneg = slots("x")
        nc.scalar.activation(out=sneg[:], in_=px[:], func=ACT.Copy, scale=iz2[:, 1:2])
        an = column("an")
        nc.scalar.activation(out=an[:], in_=an2[:], func=ACT.Copy, scale=iz2[:, 0:1])
        h = slots("h")
        hsum = column("hsum")
        nc.vector.scalar_tensor_tensor(
            out=h[:], in0=sq2[:], scalar=iz[:], in1=wpu[:], op0=ALU.mult, op1=ALU.mult, accum_out=hsum[:]
        )
        e1 = slots("e1")
        nc.vector.scalar_tensor_tensor(out=e1[:], in0=pu[:], scalar=an[:], in1=h[:], op0=ALU.mult, op1=ALU.add)
        n = slots("n")
        nc.scalar.activation(out=n[:], in_=sneg[:], func=ACT.Copy, scale=hsum[:])
        nc.vector.tensor_tensor(out=window[:].indirect(offsets[:]), in0=e1[:], in1=n[:], op=ALU.add)

        for k in range(len(OUT_CUTS) - 1):
            cols = slice(OUT_CUTS[k], OUT_CUTS[k + 1])
            res = keep.tile([P, OUT_CUTS[k + 1] - OUT_CUTS[k]], F32, name="res%d" % k)
            nc.vector.tensor_tensor(out=res[:], in0=window[:, cols], in1=base_sb[:, cols], op=ALU.add)
            nc.sync.dma_start(out=out[:, cols], in_=res[:])
